import numpy as np
import ml_dtypes


def mxq(x, axis, fmt="e4m3"):
    dtype, down = {"e4m3": (ml_dtypes.float8_e4m3fn, 7), "e5m2": (ml_dtypes.float8_e5m2, 14)}[fmt]
    v = np.moveaxis(np.asarray(x, np.float32).astype(ml_dtypes.bfloat16).astype(np.float64), axis, -1)
    blocks = v.reshape(v.shape[:-1] + (-1, 32))
    amax = np.abs(blocks).max(-1, keepdims=True)
    byte = np.maximum(np.where(amax > 0, np.frexp(amax)[1] - 1 + 127, 0) - down, 1)
    scale = np.exp2(byte - 127.0)
    codes = (blocks / scale).astype(np.float32).astype(dtype).astype(np.float64)
    return np.moveaxis((codes * scale).reshape(v.shape), -1, axis)


WIDE = False


def mx_kscale(k):
    if not WIDE:
        return np.ones(k)
    levels = np.array([10, -10, 5, -5, 0])
    if k % 512:
        return np.exp2(np.random.permutation(np.resize(levels, k // 32))).repeat(32)
    a = np.empty((k // 512, 16))
    for p in range(k // 512):
        a[p, :8] = np.random.permutation(np.resize(levels, 8))
        for g in range(8):
            far = levels[np.abs(levels - a[p, g]) >= 10]
            a[p, g + 8] = far[np.random.randint(len(far))]
    return np.exp2(a.ravel()).repeat(32)


def f64(x):
    return np.asarray(x).astype(np.float64)


def striped(idx):
    return np.tile(idx.reshape(-1, 16).T, (8, 1)).astype(np.uint16)


def unstriped(offs):
    return offs[:16].T.reshape(-1).astype(np.int64)


def striped8(idx):
    return np.concatenate([v.reshape(-1, 16).T for v in idx]).astype(np.uint16)


def unstriped8(offs):
    return np.stack([offs[16 * g:16 * g + 16].T.reshape(-1) for g in range(8)]).astype(np.int64)


E2M1 = np.array([0.0, 0.5, 1.0, 1.5, 2.0, 3.0, 4.0, 6.0, -0.0, -0.5, -1.0, -1.5, -2.0, -3.0, -4.0, -6.0])


def pack_weight(w, fmt):
    k, n = w.shape
    w = f64(np.asarray(w, np.float32).astype(ml_dtypes.bfloat16)).reshape(k // 32, 32, n)
    amax = np.abs(w).max(1)
    if fmt == "e4m3":
        byte = np.frexp(amax)[1] - 1 + 127 - 7
    else:
        mant, ex = np.frexp(amax / 6.0)
        byte = np.where(mant > 0.5, ex, ex - 1) + 127
    byte = np.clip(np.where(amax > 0, byte, 1), 1, 254)
    scaled = (w * np.exp2(127.0 - byte)[:, None, :]).reshape(k, n).astype(np.float32)
    by_word = np.ascontiguousarray(scaled.reshape(k // 512, 128, 4, n).transpose(0, 1, 3, 2))
    if fmt == "e4m3":
        words = by_word.astype(ml_dtypes.float8_e4m3fn).view(np.uint8)
    else:
        c = by_word.astype(ml_dtypes.float4_e2m1fn).view(np.uint8) & 0xF
        words = (c[..., 0::2] | (c[..., 1::2] << 4)).reshape(k // 512, 128, 2 * n)
    return np.ascontiguousarray(words), np.ascontiguousarray(byte.astype(np.uint8).reshape(k // 512, 16, n))


def unpack_weight(words, scales, fmt):
    g, _, n = scales.shape
    words = np.ascontiguousarray(words).reshape(g, 128, n, -1)
    if fmt == "e4m3":
        vals = words.view(ml_dtypes.float8_e4m3fn).astype(np.float64)
    else:
        nib = np.empty((g, 128, n, 4), np.uint8)
        nib[..., 0::2] = words & 0xF
        nib[..., 1::2] = words >> 4
        vals = E2M1[nib]
    vals = vals * np.repeat(np.exp2(scales.astype(np.float64) - 127.0), 8, axis=1)[..., None]
    return vals.transpose(0, 1, 3, 2).reshape(g * 512, n)


def pack_table(v):
    words, scales = pack_weight(v, "e4m3")
    return np.concatenate([words.reshape(words.shape[0], -1), scales.reshape(scales.shape[0], -1)], axis=1)


def unpack_table(tab):
    g, t = tab.shape[0], tab.shape[1] // 528
    return unpack_weight(tab[:, :512 * t].reshape(g, 128, t, 4), tab[:, 512 * t:].reshape(g, 16, t), "e4m3")


def gelu(v):
    return 0.5 * v * (1.0 + np.tanh(np.sqrt(2.0 / np.pi) * (v + 0.044715 * v**3)))


K, M, T, S = 1536, 512, 512, 256


def setup_inputs():
    n = np.random.standard_normal
    s = mx_kscale(K)[:, None]
    return {
        "tab": pack_table(n((K, T)) * s),
        "w": (n((K, M)) / np.sqrt(K) / s).astype(np.float32),
        "b": (0.3 * n(512)).astype(np.float32),
        "wgo": np.repeat(np.random.uniform(0.5, 2.0, (8, S)), 16, axis=0).astype(np.float32),
        "offs": striped(np.random.permutation(T)[:S]),
        "offs2": striped8(np.stack([np.random.permutation(T)[:S] for _ in range(8)])),
    }


def reference(tab, w, b, wgo, offs, offs2):
    tab_ = unpack_table(tab)[:, unstriped(offs)]
    w_ = mxq(f64(w), 0, "e4m3")
    y = w_.T @ tab_
    place = unstriped8(offs2)[np.arange(M) % 128 // 16]
    out = np.zeros((M, T))
    out[np.arange(M)[:, None], place] = f64(wgo)[np.arange(M) % 128] * (gelu(y + f64(b)[:, None]))
    return out

@@ -1,0 +1,144 @@
+from contextlib import ExitStack
+
+import concourse.mybir as mybir
+
+K, M, T, S = 1536, 512, 512, 256
+FLOPS = 2 * K * M * S
+
+F32 = mybir.dt.float32
+BF16 = mybir.dt.bfloat16
+I32 = mybir.dt.int32
+U32 = mybir.dt.uint32
+U16 = mybir.dt.uint16
+U8 = mybir.dt.uint8
+FP8X4 = mybir.dt.float8_e4m3fn_x4
+MULT = mybir.AluOpType.mult
+GELU = mybir.ActivationFunctionType.Gelu_apprx_tanh
+
+P = 128
+PASSES = K // 512
+TILES = M // P
+WORD_BYTES = 512 * T
+ON_VECTOR = ((0, 2), (1, 1), (3, 2))
+
+
+def tile_list_tabhs_gelu_kernel(tc, tab, w, b, wgo, offs, offs2, out):
+    nc = tc.nc
+    with ExitStack() as ctx:
+        keep = ctx.enter_context(tc.tile_pool(name="keep", bufs=1))
+        psum = ctx.enter_context(tc.psum_pool(name="psum", bufs=1))
+
+        pick = keep.tile([P, S // 16], U16, name="pick")
+        place = keep.tile([P, S // 16], U16, name="place")
+        words = [keep.tile([P, T], I32, name=f"words{a}", align_bytes=64) for a in range(PASSES)]
+        scales = keep.tile([P, T // 4], I32, name="scales", align_bytes=64)
+        bias = keep.tile([P, TILES], F32, name="bias")
+        weight = keep.tile([P, S], F32, name="weight")
+        raw = [[keep.tile([P, 4, P], F32, name=f"raw{m}_{a}") for a in range(PASSES)] for m in range(TILES)]
+        grouped = [keep.tile([P, PASSES, P, 4], BF16, name=f"grouped{m}", align_bytes=64) for m in range(TILES)]
+        codes = [keep.tile([P, PASSES * P], U32, name=f"codes{m}", align_bytes=64) for m in range(TILES)]
+        cscales = [keep.tile([P, PASSES * P], U8, name=f"cscales{m}", align_bytes=64) for m in range(TILES)]
+        pwords = [keep.tile([P, S], U32, name=f"pwords{a}", align_bytes=64) for a in range(PASSES)]
+        pscales = keep.tile([P, S], U8, name="pscales", align_bytes=64)
+        result = [keep.tile([P, S], F32, name=f"result{m}") for m in range(TILES)]
+        placed = [keep.tile([P, T], F32, name=f"placed{m}") for m in range(TILES)]
+        warm = keep.tile([P, 1], F32, name="warm")
+        acc = [psum.tile([P, S], F32, name=f"acc{m}") for m in range(TILES)]
+
+        def load_words(a):
+            nc.sync.dma_start(words[a][:], tab[a, 0:WORD_BYTES].bitcast(I32).rearrange("(p t) -> p t", p=P))
+
+        def load_w(m, a):
+            src = w[512 * a : 512 * (a + 1), P * m : P * (m + 1)]
+            nc.sync.dma_start(raw[m][a][:], src.rearrange("(p j) n -> p j n", j=4))
+
+        nc.vector.memset(scales[:], 0)
+        nc.gpsimd.memset(warm[:], 0.0)
+        for m in range(TILES):
+            nc.vector.memset(placed[m][:], 0.0)
+        nc.sync.dma_start(pick[:], offs)
+        load_words(0)
+        load_w(0, 0)
+        load_words(1)
+        load_w(0, 1)
+        load_words(2)
+        load_w(0, 2)
+        nc.sync.dma_start(place[:], offs2)
+        for q in range(4):
+            lo = WORD_BYTES + 4 * T * q
+            src = tab[:, lo : lo + 4 * T].bitcast(I32).rearrange("a (r t) -> a r t", r=4)
+            nc.scalar.dma_start(scales[32 * q : 32 * q + 4 * PASSES, :], src)
+        nc.gpsimd.dma_start(weight[:], wgo)
+        with nc.allow_non_contiguous_dma(reason="one bias value a partition"):
+            nc.gpsimd.dma_start(bias[:], b.rearrange("(c p) -> p c", p=P))
+        nc.scalar.activation(warm[:], warm[:], GELU)
+        for m in range(1, TILES):
+            for a in range(PASSES):
+                load_w(m, a)
+
+        def pick_words(a):
+            nc.vector.tensor_copy(pwords[a][:], words[a][:].bitcast(U32).indirect(pick[:]))
+
+        def group(eng, m, a):
+            dst = grouped[m][:, a, :, :].rearrange("p (c i) t -> p c t i", i=4)
+            src = raw[m][a][:].rearrange("p t (c i) -> p c t i", i=4)
+            if eng == "s":
+                nc.scalar.copy(dst, src)
+            else:
+                nc.vector.tensor_copy(dst, src)
+
+        def quantize(m, a0, a1):
+            cols = slice(P * a0, P * a1)
+            nc.vector.quantize_mx(
+                out=codes[m][:, cols].bitcast(FP8X4),
+                scales=cscales[m][:, cols],
+                in_=grouped[m][:].rearrange("p a c t -> p (a c t)")[:, 512 * a0 : 512 * a1],
+            )
+
+        def multiply(m):
+            for a in range(PASSES):
+                cols = slice(P * a, P * (a + 1))
+                nc.tensor.matmul_mx(
+                    out=acc[m][:],
+                    lhsT=codes[m][:, cols].bitcast(FP8X4),
+                    lhsT_scale=cscales[m][:, cols],
+                    rhs=pwords[a][:].bitcast(FP8X4),
+                    rhs_scale=pscales[4 * a : P, :],
+                    start=(a == 0),
+                    stop=(a == PASSES - 1),
+                )
+
+        def gelu(m):
+            nc.scalar.activation(result[m][:], acc[m][:], GELU, bias=bias[:, m : m + 1])
+
+        def scatter(m, h):
+            cols = slice(P * h, P * (h + 1))
+            nc.vector.tensor_tensor(
+                placed[m][:].indirect(place[:, 8 * h : 8 * (h + 1)]), result[m][:, cols], weight[:, cols], MULT
+            )
+
+        def store(m):
+            nc.sync.dma_start(out[P * m : P * (m + 1), :], placed[m][:])
+
+        pick_words(0)
+        group("s", 0, 0)
+        pick_words(1)
+        group("s", 0, 1)
+        pick_words(2)
+        nc.vector.tensor_copy(pscales[:], scales[:].bitcast(U8).indirect(pick[:]))
+        for m in range(TILES):
+            for a in range(PASSES):
+                if m + a > 0 and (m, a) != (0, 1):
+                    group("v" if (m, a) in ON_VECTOR else "s", m, a)
+            quantize(m, 0, 2)
+            quantize(m, 2, 3)
+            multiply(m)
+            if m > 0:
+                gelu(m - 1)
+                scatter(m - 1, 0)
+                scatter(m - 1, 1)
+                store(m - 1)
+        gelu(TILES - 1)
+        scatter(TILES - 1, 0)
+        scatter(TILES - 1, 1)
+        store(TILES - 1)

@@ -1,6 +1,7 @@
 from contextlib import ExitStack
 
 import concourse.mybir as mybir
+from concourse.masks import make_identity
 
 K, M, T, S = 1536, 512, 512, 256
 FLOPS = 2 * K * M * S
@@ -19,7 +20,7 @@ P = 128
 PASSES = K // 512
 TILES = M // P
 WORD_BYTES = 512 * T
-ON_VECTOR = ((0, 2), (1, 1), (3, 2))
+BLOCKS = ((0, 256), (256, 256))
 
 
 def tile_list_tabhs_gelu_kernel(tc, tab, w, b, wgo, offs, offs2, out):
@@ -32,76 +33,63 @@ def tile_list_tabhs_gelu_kernel(tc, tab, w, b, wgo, offs, offs2, out):
         place = keep.tile([P, S // 16], U16, name="place")
         words = [keep.tile([P, T], I32, name=f"words{a}", align_bytes=64) for a in range(PASSES)]
         scales = keep.tile([P, T // 4], I32, name="scales", align_bytes=64)
+        brows = keep.tile([P, P], F32, name="brows")
+        ident = keep.tile([P, P], F32, name="ident")
         bias = keep.tile([P, TILES], F32, name="bias")
         weight = keep.tile([P, S], F32, name="weight")
-        raw = [[keep.tile([P, 4, P], F32, name=f"raw{m}_{a}") for a in range(PASSES)] for m in range(TILES)]
-        grouped = [keep.tile([P, PASSES, P, 4], BF16, name=f"grouped{m}", align_bytes=64) for m in range(TILES)]
-        codes = [keep.tile([P, PASSES * P], U32, name=f"codes{m}", align_bytes=64) for m in range(TILES)]
-        cscales = [keep.tile([P, PASSES * P], U8, name=f"cscales{m}", align_bytes=64) for m in range(TILES)]
+        raw = [[keep.tile([P, 4, n], F32, name=f"raw{k}_{a}") for a in range(PASSES)] for k, (c0, n) in enumerate(BLOCKS)]
+        grouped = [keep.tile([P, PASSES, n, 4], BF16, name=f"grouped{k}", align_bytes=64) for k, (c0, n) in enumerate(BLOCKS)]
+        codes = [keep.tile([P, PASSES * n], U32, name=f"codes{k}", align_bytes=64) for k, (c0, n) in enumerate(BLOCKS)]
+        cscales = [keep.tile([P, PASSES * n], U8, name=f"cscales{k}", align_bytes=64) for k, (c0, n) in enumerate(BLOCKS)]
         pwords = [keep.tile([P, S], U32, name=f"pwords{a}", align_bytes=64) for a in range(PASSES)]
         pscales = keep.tile([P, S], U8, name="pscales", align_bytes=64)
         result = [keep.tile([P, S], F32, name=f"result{m}") for m in range(TILES)]
         placed = [keep.tile([P, T], F32, name=f"placed{m}") for m in range(TILES)]
         warm = keep.tile([P, 1], F32, name="warm")
+        bcols = psum.tile([P, P], F32, name="bcols")
         acc = [psum.tile([P, S], F32, name=f"acc{m}") for m in range(TILES)]
 
         def load_words(a):
             nc.sync.dma_start(words[a][:], tab[a, 0:WORD_BYTES].bitcast(I32).rearrange("(p t) -> p t", p=P))
 
-        def load_w(m, a):
-            src = w[512 * a : 512 * (a + 1), P * m : P * (m + 1)]
-            nc.sync.dma_start(raw[m][a][:], src.rearrange("(p j) n -> p j n", j=4))
-
-        nc.vector.memset(scales[:], 0)
-        nc.gpsimd.memset(warm[:], 0.0)
-        for m in range(TILES):
-            nc.vector.memset(placed[m][:], 0.0)
-        nc.sync.dma_start(pick[:], offs)
-        load_words(0)
-        load_w(0, 0)
-        load_words(1)
-        load_w(0, 1)
-        load_words(2)
-        load_w(0, 2)
-        nc.sync.dma_start(place[:], offs2)
-        for q in range(4):
-            lo = WORD_BYTES + 4 * T * q
-            src = tab[:, lo : lo + 4 * T].bitcast(I32).rearrange("a (r t) -> a r t", r=4)
-            nc.scalar.dma_start(scales[32 * q : 32 * q + 4 * PASSES, :], src)
-        nc.gpsimd.dma_start(weight[:], wgo)
-        with nc.allow_non_contiguous_dma(reason="one bias value a partition"):
-            nc.gpsimd.dma_start(bias[:], b.rearrange("(c p) -> p c", p=P))
-        nc.scalar.activation(warm[:], warm[:], GELU)
-        for m in range(1, TILES):
-            for a in range(PASSES):
-                load_w(m, a)
+        def load_w(k, a):
+            c0, n = BLOCKS[k]
+            src = w[512 * a : 512 * (a + 1), c0 : c0 + n]
+            nc.sync.dma_start(raw[k][a][:], src.rearrange("(p j) n -> p j n", j=4))
 
         def pick_words(a):
             nc.vector.tensor_copy(pwords[a][:], words[a][:].bitcast(U32).indirect(pick[:]))
 
-        def group(eng, m, a):
-            dst = grouped[m][:, a, :, :].rearrange("p (c i) t -> p c t i", i=4)
-            src = raw[m][a][:].rearrange("p t (c i) -> p c t i", i=4)
+        def pick_scales():
+            nc.vector.tensor_copy(pscales[:], scales[:].bitcast(U8).indirect(pick[:]))
+
+        def group(eng, k, a, lo, hi):
+            dst = grouped[k][:, a, lo:hi, :].rearrange("p (c i) t -> p c t i", i=4)
+            src = raw[k][a][:, :, lo:hi].rearrange("p t (c i) -> p c t i", i=4)
             if eng == "s":
                 nc.scalar.copy(dst, src)
             else:
                 nc.vector.tensor_copy(dst, src)
 
-        def quantize(m, a0, a1):
-            cols = slice(P * a0, P * a1)
+        def quantize(k, a, lo, hi):
+            n = BLOCKS[k][1]
+            cols = slice(n * a + lo, n * a + hi)
             nc.vector.quantize_mx(
-                out=codes[m][:, cols].bitcast(FP8X4),
-                scales=cscales[m][:, cols],
-                in_=grouped[m][:].rearrange("p a c t -> p (a c t)")[:, 512 * a0 : 512 * a1],
+                out=codes[k][:, cols].bitcast(FP8X4),
+                scales=cscales[k][:, cols],
+                in_=grouped[k][:].rearrange("p a c t -> p (a c t)")[:, 4 * (n * a + lo) : 4 * (n * a + hi)],
             )
 
         def multiply(m):
+            k = [i for i, (c0, n) in enumerate(BLOCKS) if c0 <= P * m < c0 + n][0]
+            c0, n = BLOCKS[k]
             for a in range(PASSES):
-                cols = slice(P * a, P * (a + 1))
+                lo = n * a + P * m - c0
+                cols = slice(lo, lo + P)
                 nc.tensor.matmul_mx(
                     out=acc[m][:],
-                    lhsT=codes[m][:, cols].bitcast(FP8X4),
-                    lhsT_scale=cscales[m][:, cols],
+                    lhsT=codes[k][:, cols].bitcast(FP8X4),
+                    lhsT_scale=cscales[k][:, cols],
                     rhs=pwords[a][:].bitcast(FP8X4),
                     rhs_scale=pscales[4 * a : P, :],
                     start=(a == 0),
@@ -120,25 +108,66 @@ def tile_list_tabhs_gelu_kernel(tc, tab, w, b, wgo, offs, offs2, out):
         def store(m):
             nc.sync.dma_start(out[P * m : P * (m + 1), :], placed[m][:])
 
-        pick_words(0)
-        group("s", 0, 0)
-        pick_words(1)
-        group("s", 0, 1)
-        pick_words(2)
-        nc.vector.tensor_copy(pscales[:], scales[:].bitcast(U8).indirect(pick[:]))
+        nc.vector.memset(scales[:], 0)
+        nc.gpsimd.memset(warm[:], 0.0)
+        nc.gpsimd.memset(brows[:], 0.0)
         for m in range(TILES):
+            nc.vector.memset(placed[m][:], 0.0)
+        load_words(0)
+        nc.sync.dma_start(pick[:], offs)
+        load_w(0, 0)
+        load_words(1)
+        load_w(0, 1)
+        load_words(2)
+        load_w(0, 2)
+        nc.sync.dma_start(place[:], offs2)
+        for q in range(4):
+            lo = WORD_BYTES + 4 * T * q
+            src = tab[:, lo : lo + 4 * T].bitcast(I32).rearrange("a (r t) -> a r t", r=4)
+            nc.scalar.dma_start(scales[32 * q : 32 * q + 4 * PASSES, :], src)
+        nc.scalar.activation(warm[:], warm[:], GELU)
+        nc.gpsimd.dma_start(brows[0:TILES, :], b.rearrange("(m p) -> m p", p=P))
+        nc.gpsimd.dma_start(weight[:], wgo)
+        make_identity(nc, ident[:])
+        nc.tensor.transpose(bcols[:], brows[:], ident[:])
+        nc.scalar.copy(bias[:], bcols[:, 0:TILES])
+        for k in range(1, len(BLOCKS)):
             for a in range(PASSES):
-                if m + a > 0 and (m, a) != (0, 1):
-                    group("v" if (m, a) in ON_VECTOR else "s", m, a)
-            quantize(m, 0, 2)
-            quantize(m, 2, 3)
-            multiply(m)
-            if m > 0:
-                gelu(m - 1)
-                scatter(m - 1, 0)
-                scatter(m - 1, 1)
-                store(m - 1)
-        gelu(TILES - 1)
-        scatter(TILES - 1, 0)
-        scatter(TILES - 1, 1)
-        store(TILES - 1)
+                load_w(k, a)
+
+        pick_words(0)
+        group("s", 0, 0, 0, 256)
+        pick_words(1)
+        group("s", 0, 1, 0, 256)
+        pick_scales()
+        pick_words(2)
+        quantize(0, 0, 0, 256)
+        quantize(0, 1, 0, 256)
+        group("v", 0, 2, 0, 128)
+        group("s", 0, 2, 128, 256)
+        quantize(0, 2, 0, 128)
+        multiply(0)
+        quantize(0, 2, 128, 256)
+        multiply(1)
+        gelu(0)
+        gelu(1)
+        group("s", 1, 0, 0, 256)
+        group("v", 1, 1, 0, 128)
+        group("s", 1, 1, 128, 256)
+        group("v", 1, 2, 0, 128)
+        group("s", 1, 2, 128, 256)
+        scatter(0, 0)
+        scatter(0, 1)
+        store(0)
+        quantize(1, 0, 0, 256)
+        quantize(1, 1, 0, 256)
+        quantize(1, 2, 0, 128)
+        multiply(2)
+        gelu(2)
+        quantize(1, 2, 128, 256)
+        multiply(3)
+        gelu(3)
+        for m in range(1, TILES):
+            scatter(m, 0)
+            scatter(m, 1)
+            store(m)

from contextlib import ExitStack

import concourse.mybir as mybir
from concourse.masks import make_identity

K, M, T, S = 1536, 512, 512, 256
FLOPS = 2 * K * M * S

F32 = mybir.dt.float32
BF16 = mybir.dt.bfloat16
I32 = mybir.dt.int32
U32 = mybir.dt.uint32
U16 = mybir.dt.uint16
U8 = mybir.dt.uint8
FP8X4 = mybir.dt.float8_e4m3fn_x4
MULT = mybir.AluOpType.mult
GELU = mybir.ActivationFunctionType.Gelu_apprx_tanh

P = 128
PASSES = K // 512
TILES = M // P
WORD_BYTES = 512 * T
BLOCKS = ((0, 256), (256, 256))


def tile_list_tabhs_gelu_kernel(tc, tab, w, b, wgo, offs, offs2, out):
    nc = tc.nc
    with ExitStack() as ctx:
        keep = ctx.enter_context(tc.tile_pool(name="keep", bufs=1))
        psum = ctx.enter_context(tc.psum_pool(name="psum", bufs=1))

        pick = keep.tile([P, S // 16], U16, name="pick")
        place = keep.tile([P, S // 16], U16, name="place")
        words = [keep.tile([P, T], I32, name=f"words{a}", align_bytes=64) for a in range(PASSES)]
        scales = keep.tile([P, T // 4], I32, name="scales", align_bytes=64)
        brows = keep.tile([P, P], F32, name="brows")
        ident = keep.tile([P, P], F32, name="ident")
        bias = keep.tile([P, TILES], F32, name="bias")
        weight = keep.tile([P, S], F32, name="weight")
        raw = [[keep.tile([P, 4, n], F32, name=f"raw{k}_{a}") for a in range(PASSES)] for k, (c0, n) in enumerate(BLOCKS)]
        grouped = [keep.tile([P, PASSES, n, 4], BF16, name=f"grouped{k}", align_bytes=64) for k, (c0, n) in enumerate(BLOCKS)]
        codes = [keep.tile([P, PASSES * n], U32, name=f"codes{k}", align_bytes=64) for k, (c0, n) in enumerate(BLOCKS)]
        cscales = [keep.tile([P, PASSES * n], U8, name=f"cscales{k}", align_bytes=64) for k, (c0, n) in enumerate(BLOCKS)]
        pwords = [keep.tile([P, S], U32, name=f"pwords{a}", align_bytes=64) for a in range(PASSES)]
        pscales = keep.tile([P, S], U8, name="pscales", align_bytes=64)
        result = [keep.tile([P, S], F32, name=f"result{m}") for m in range(TILES)]
        placed = [keep.tile([P, T], F32, name=f"placed{m}") for m in range(TILES)]
        warm = keep.tile([P, 1], F32, name="warm")
        bcols = psum.tile([P, P], F32, name="bcols")
        acc = [psum.tile([P, S], F32, name=f"acc{m}") for m in range(TILES)]

        def load_words(a):
            nc.sync.dma_start(words[a][:], tab[a, 0:WORD_BYTES].bitcast(I32).rearrange("(p t) -> p t", p=P))

        def load_w(k, a):
            c0, n = BLOCKS[k]
            src = w[512 * a : 512 * (a + 1), c0 : c0 + n]
            nc.sync.dma_start(raw[k][a][:], src.rearrange("(p j) n -> p j n", j=4))

        def pick_words(a):
            nc.vector.tensor_copy(pwords[a][:], words[a][:].bitcast(U32).indirect(pick[:]))

        def pick_scales():
            nc.vector.tensor_copy(pscales[:], scales[:].bitcast(U8).indirect(pick[:]))

        def group(eng, k, a, lo, hi):
            dst = grouped[k][:, a, lo:hi, :].rearrange("p (c i) t -> p c t i", i=4)
            src = raw[k][a][:, :, lo:hi].rearrange("p t (c i) -> p c t i", i=4)
            if eng == "s":
                nc.scalar.copy(dst, src)
            else:
                nc.vector.tensor_copy(dst, src)

        def quantize(k, a, lo, hi):
            n = BLOCKS[k][1]
            cols = slice(n * a + lo, n * a + hi)
            nc.vector.quantize_mx(
                out=codes[k][:, cols].bitcast(FP8X4),
                scales=cscales[k][:, cols],
                in_=grouped[k][:].rearrange("p a c t -> p (a c t)")[:, 4 * (n * a + lo) : 4 * (n * a + hi)],
            )

        def multiply(m):
            k = [i for i, (c0, n) in enumerate(BLOCKS) if c0 <= P * m < c0 + n][0]
            c0, n = BLOCKS[k]
            for a in range(PASSES):
                lo = n * a + P * m - c0
                cols = slice(lo, lo + P)
                nc.tensor.matmul_mx(
                    out=acc[m][:],
                    lhsT=codes[k][:, cols].bitcast(FP8X4),
                    lhsT_scale=cscales[k][:, cols],
                    rhs=pwords[a][:].bitcast(FP8X4),
                    rhs_scale=pscales[4 * a : P, :],
                    start=(a == 0),
                    stop=(a == PASSES - 1),
                )

        def gelu(m):
            nc.scalar.activation(result[m][:], acc[m][:], GELU, bias=bias[:, m : m + 1])

        def scatter(m, h):
            cols = slice(P * h, P * (h + 1))
            nc.vector.tensor_tensor(
                placed[m][:].indirect(place[:, 8 * h : 8 * (h + 1)]), result[m][:, cols], weight[:, cols], MULT
            )

        def store(m):
            nc.sync.dma_start(out[P * m : P * (m + 1), :], placed[m][:])

        nc.vector.memset(scales[:], 0)
        nc.gpsimd.memset(warm[:], 0.0)
        nc.gpsimd.memset(brows[:], 0.0)
        for m in range(TILES):
            nc.vector.memset(placed[m][:], 0.0)
        load_words(0)
        nc.sync.dma_start(pick[:], offs)
        load_w(0, 0)
        load_words(1)
        load_w(0, 1)
        load_words(2)
        load_w(0, 2)
        nc.sync.dma_start(place[:], offs2)
        for q in range(4):
            lo = WORD_BYTES + 4 * T * q
            src = tab[:, lo : lo + 4 * T].bitcast(I32).rearrange("a (r t) -> a r t", r=4)
            nc.scalar.dma_start(scales[32 * q : 32 * q + 4 * PASSES, :], src)
        nc.scalar.activation(warm[:], warm[:], GELU)
        nc.gpsimd.dma_start(brows[0:TILES, :], b.rearrange("(m p) -> m p", p=P))
        nc.gpsimd.dma_start(weight[:], wgo)
        make_identity(nc, ident[:])
        nc.tensor.transpose(bcols[:], brows[:], ident[:])
        nc.scalar.copy(bias[:], bcols[:, 0:TILES])
        for k in range(1, len(BLOCKS)):
            for a in range(PASSES):
                load_w(k, a)

        pick_words(0)
        group("s", 0, 0, 0, 256)
        pick_words(1)
        group("s", 0, 1, 0, 256)
        pick_scales()
        pick_words(2)
        quantize(0, 0, 0, 256)
        quantize(0, 1, 0, 256)
        group("v", 0, 2, 0, 128)
        group("s", 0, 2, 128, 256)
        quantize(0, 2, 0, 128)
        multiply(0)
        quantize(0, 2, 128, 256)
        multiply(1)
        gelu(0)
        gelu(1)
        group("s", 1, 0, 0, 256)
        group("v", 1, 1, 0, 128)
        group("s", 1, 1, 128, 256)
        group("v", 1, 2, 0, 128)
        group("s", 1, 2, 128, 256)
        scatter(0, 0)
        scatter(0, 1)
        store(0)
        quantize(1, 0, 0, 256)
        quantize(1, 1, 0, 256)
        quantize(1, 2, 0, 128)
        multiply(2)
        gelu(2)
        quantize(1, 2, 128, 256)
        multiply(3)
        gelu(3)
        for m in range(1, TILES):
            scatter(m, 0)
            scatter(m, 1)
            store(m)
